import numpy as np
import ml_dtypes


def mxq(x, axis, fmt="e4m3"):
    dtype, down = {"e4m3": (ml_dtypes.float8_e4m3fn, 7), "e5m2": (ml_dtypes.float8_e5m2, 14)}[fmt]
    v = np.moveaxis(np.asarray(x, np.float32).astype(ml_dtypes.bfloat16).astype(np.float64), axis, -1)
    blocks = v.reshape(v.shape[:-1] + (-1, 32))
    amax = np.abs(blocks).max(-1, keepdims=True)
    byte = np.maximum(np.where(amax > 0, np.frexp(amax)[1] - 1 + 127, 0) - down, 1)
    scale = np.exp2(byte - 127.0)
    codes = (blocks / scale).astype(np.float32).astype(dtype).astype(np.float64)
    return np.moveaxis((codes * scale).reshape(v.shape), -1, axis)


WIDE = False


def mx_kscale(k):
    if not WIDE:
        return np.ones(k)
    levels = np.array([10, -10, 5, -5, 0])
    if k % 512:
        return np.exp2(np.random.permutation(np.resize(levels, k // 32))).repeat(32)
    a = np.empty((k // 512, 16))
    for p in range(k // 512):
        a[p, :8] = np.random.permutation(np.resize(levels, 8))
        for g in range(8):
            far = levels[np.abs(levels - a[p, g]) >= 10]
            a[p, g + 8] = far[np.random.randint(len(far))]
    return np.exp2(a.ravel()).repeat(32)


def f64(x):
    return np.asarray(x).astype(np.float64)


def striped(idx):
    return np.tile(idx.reshape(-1, 16).T, (8, 1)).astype(np.uint16)


def unstriped(offs):
    return offs[:16].T.reshape(-1).astype(np.int64)


def striped8(idx):
    return np.concatenate([x.reshape(-1, 16).T for x in idx]).astype(np.uint16)


def runs(offs, k):
    lists = np.stack([offs[16 * r : 16 * r + 16].T.reshape(-1) for r in range(8)]).astype(np.int64)
    return lists[np.arange(k) % 512 // 64]


def pack_weight(w):
    k, n = w.shape
    w = f64(np.asarray(w, np.float32).astype(ml_dtypes.bfloat16)).reshape(k // 32, 32, n)
    amax = np.abs(w).max(1)
    byte = np.clip(np.where(amax > 0, np.frexp(amax)[1] - 1 + 127 - 7, 1), 1, 254)
    scaled = (w * np.exp2(127.0 - byte)[:, None, :]).reshape(k, n).astype(np.float32)
    words = np.ascontiguousarray(scaled.reshape(k // 512, 128, 4, n).transpose(0, 1, 3, 2)).astype(ml_dtypes.float8_e4m3fn).view(np.uint8)
    return words, np.ascontiguousarray(byte.astype(np.uint8).reshape(k // 512, 16, n))


def unpack_weight(words, scales):
    g, p, n, _ = words.shape
    vals = np.ascontiguousarray(words).view(ml_dtypes.float8_e4m3fn).astype(np.float64) * np.repeat(np.exp2(scales.astype(np.float64) - 127.0), 8, axis=1)[..., None]
    return vals.transpose(0, 1, 3, 2).reshape(g * 512, n)


def sigmoid(v):
    return 1.0 / (1.0 + np.exp(-np.maximum(v, -700.0)))


K, T, S, V, H, J = 512, 2048, 512, 256, 512, 512


def setup_inputs():
    n = np.random.standard_normal
    s = mx_kscale(K)[:, None]
    u = mx_kscale(S)
    packed_xT = pack_weight(n((K, T)) * s)
    return {
        "x_words": packed_xT[0],
        "x_scales": packed_xT[1],
        "w1": (n((K, H)) / np.sqrt(K) / s).astype(np.float32),
        "w2": (n((K, H)) / np.sqrt(K) / s).astype(np.float32),
        "w3": (n((K, H)) / np.sqrt(K) / s).astype(np.float32),
        "ga": (np.random.uniform(0.5, 1.5, (H, 1)) * u[:, None]).astype(np.float32),
        "gb": (np.random.uniform(0.5, 1.5, (H, 1)) / u[:, None]).astype(np.float32),
        "tab": n((S, J)).astype(np.float32),
        "offs": striped(np.random.permutation(T)[:S]),
        "two": striped(np.random.permutation(T)[:S]),
        "n1": striped(np.random.permutation(S)),
        "n2": striped(np.random.permutation(S)),
        "three": striped(np.random.permutation(T)[:V]),
        "n3": striped8(np.stack([np.random.permutation(V) for _ in range(8)])),
        "n4": striped8(np.stack([np.random.permutation(V) for _ in range(8)])),
        "n5": striped8(np.stack([np.random.permutation(V) for _ in range(8)])),
        "n6": striped8(np.random.randint(0, J, (8, V))),
        "n7": striped8(np.random.randint(0, J, (8, V))),
        "n8": striped8(np.stack([np.random.permutation(V) for _ in range(8)])),
    }


def reference(x_words, x_scales, w1, w2, w3, ga, gb, tab, offs, two, n1, n2, three, n3, n4, n5, n6, n7, n8):
    xq = unpack_weight(x_words, x_scales)[:, unstriped(offs)]
    y = mxq(f64(w1), 0, "e4m3").T @ xq
    x_two = unpack_weight(x_words, x_scales)[:, unstriped(two)]
    d = mxq(f64(w2), 0, "e4m3").T @ x_two
    z = f64(ga) * ((y - y[:, unstriped(n1)]) / (np.abs(d) + np.abs(d[:, unstriped(n2)]) + 0.5))
    x_three = unpack_weight(x_words, x_scales)[:, unstriped(three)]
    b = mxq(f64(w3), 0, "e4m3").T @ x_three
    z2 = f64(gb) * ((b[np.arange(H)[:, None], runs(n3, H)]) * sigmoid(b) + (b[np.arange(H)[:, None], runs(n4, H)]) * (sigmoid(b[np.arange(H)[:, None], runs(n5, H)])))
    s = 0.0625 * ((mxq(z, 0, "e4m3").T @ mxq(z2, 0, "e4m3")))
    return (s[np.arange(S)[:, None], runs(n8, S)]) * (f64(tab)[np.arange(S)[:, None], runs(n6, S)]) + f64(tab)[np.arange(S)[:, None], runs(n7, S)]

@@ -1,0 +1,217 @@
+from contextlib import ExitStack
+
+import concourse.mybir as mybir
+from concourse.masks import make_identity
+
+F32 = mybir.dt.float32
+BF16 = mybir.dt.bfloat16
+I32 = mybir.dt.int32
+U32 = mybir.dt.uint32
+U16 = mybir.dt.uint16
+U8 = mybir.dt.uint8
+FP8X4 = mybir.dt.float8_e4m3fn_x4
+ACT = mybir.ActivationFunctionType
+ALU = mybir.AluOpType
+
+K, T, S, V, H, J = 512, 2048, 512, 256, 512, 512
+P = 128
+FLOPS = 2 * K * H * (S + S + V) + 2 * H * S * V
+
+Y_WINDOW = S + 16
+A_WINDOW = S + 192
+
+
+def tile_picked_twknormbwsumkinda_none_p_kernel(tc, x_words, x_scales, w1, w2, w3, ga, gb, tab, offs, two, n1, n2, three, n3, n4, n5, n6, n7, n8, out):
+    nc = tc.nc
+    with ExitStack() as ctx:
+        lists = ctx.enter_context(tc.tile_pool(name="lists", bufs=1))
+        keep = ctx.enter_context(tc.tile_pool(name="keep", bufs=1))
+        psum = ctx.enter_context(tc.psum_pool(name="psum", bufs=1))
+
+        def load_list(src, name):
+            lst = lists.tile([P, src.shape[1]], U16, name=name)
+            nc.sync.dma_start(lst[:], src)
+            return lst
+
+        def sb(shape, dtype, name, tag=""):
+            return keep.tile(shape, dtype, name=name, tag=tag or name, align_bytes=64)
+
+        def bank(width, name, index):
+            return psum.tile([P, width], F32, name=name, tag=f"bank{index}")
+
+        def load_weight(w, c0, c1, name):
+            raw = sb([P, 4, c1 - c0], F32, name)
+            nc.sync.dma_start(raw[:], w.rearrange("(p j) c -> p j c", j=4)[:, :, c0:c1])
+            return raw
+
+        xs = sb([P, T], U8, "xs")
+        nc.vector.memset(xs[:].bitcast(I32), 0)
+        for q in range(4):
+            nc.scalar.dma_start(xs[32 * q : 32 * q + 4, :].bitcast(I32), x_scales[0, 4 * q : 4 * q + 4, :].bitcast(I32))
+        l_three = load_list(three, "l_three")
+        l_two = load_list(two, "l_two")
+        l_offs = load_list(offs, "l_offs")
+        w3_raw = [load_weight(w3, 256 * h, 256 * h + 256, f"w3_raw{h}") for h in range(2)]
+        xw = sb([P, T], U32, "xw")
+        nc.sync.dma_start(xw[:].bitcast(I32), x_words[0].rearrange("p n t -> p (n t)").bitcast(I32))
+        l_n3 = load_list(n3, "l_n3")
+        l_n4 = load_list(n4, "l_n4")
+        l_n5 = load_list(n5, "l_n5")
+        w2_raw = load_weight(w2, 0, H, "w2_raw")
+        gb_t = sb([P, 4], F32, "gb_t")
+        nc.sync.dma_start(gb_t[:], gb.rearrange("(p t) o -> p (t o)", t=4))
+        w1_raw = load_weight(w1, 0, H, "w1_raw")
+        l_n2 = load_list(n2, "l_n2")
+        l_n1 = load_list(n1, "l_n1")
+        ga_t = sb([P, 4], F32, "ga_t")
+        with nc.allow_non_contiguous_dma(reason="one gain a partition"):
+            nc.sync.dma_start(ga_t[:], ga.rearrange("(t p) o -> p (t o)", p=P))
+        tab_t = []
+        for t in range(4):
+            rows = sb([P, J], F32, f"tab{t}")
+            nc.sync.dma_start(rows[:], tab.rearrange("(p t) c -> t p c", t=4)[t])
+            tab_t.append(rows)
+        l_n8 = load_list(n8, "l_n8")
+        l_n6 = load_list(n6, "l_n6")
+        l_n7 = load_list(n7, "l_n7")
+
+        a_win = [sb([P, A_WINDOW], F32, f"a_win{t}") for t in range(4)]
+        y_win = [sb([P, Y_WINDOW], F32, f"y_win{t}") for t in range(4)]
+        b_win = [sb([P, 2 * V], F32, f"b_win{t}") for t in range(4)]
+        g_win = [sb([P, 2 * V], F32, f"g_win{t}") for t in range(4)]
+        s_win = [sb([P, 2 * V], F32, f"s_win{t}") for t in range(4)]
+        for t in range(4):
+            nc.gpsimd.memset(b_win[t][:, V:], 0.0)
+            nc.gpsimd.memset(g_win[t][:, V:], 0.0)
+        for t in range(4):
+            nc.gpsimd.memset(a_win[t][:, S:], 0.0)
+            nc.gpsimd.memset(y_win[t][:, S:], 0.0)
+            nc.gpsimd.memset(s_win[t][:, V:], 0.0)
+        ident = sb([P, P], F32, "ident")
+        make_identity(nc, ident[:])
+        half = sb([P, 1], F32, "half")
+        nc.gpsimd.memset(half[:], 0.5)
+
+        def pick(table, lst, n, dtype, name):
+            picked_bytes = sb([P, n], dtype, name)
+            nc.vector.tensor_copy(picked_bytes[:], table[:].indirect(lst[:]))
+            return picked_bytes
+
+        def cast_plain(engine_copy, raw, name):
+            width = raw.shape[2]
+            grouped = sb([P, width, 4], BF16, name)
+            engine_copy(grouped[:].rearrange("p (c i) j -> p c j i", i=4), raw[:].rearrange("p j (c i) -> p c j i", i=4))
+            return grouped[:].rearrange("p c j -> p (c j)")
+
+        def quantise(values, name):
+            width = values.shape[1] // 4
+            words = sb([P, width], U32, name + "_w")
+            scales = sb([P, width], U8, name + "_s")
+            nc.vector.quantize_mx(out=words[:].bitcast(FP8X4), scales=scales[:], in_=values)
+            return words, scales
+
+        def product(acc, stat, c0, mov):
+            nc.tensor.matmul_mx(out=acc, lhsT=stat[0][:, c0 : c0 + P].bitcast(FP8X4), lhsT_scale=stat[1][:, c0 : c0 + P],
+                                rhs=mov[0][:].bitcast(FP8X4), rhs_scale=mov[1][:], start=True, stop=True)
+
+        def turn_and_add(first, second, name, index):
+            acc = bank(S, name, index)
+            for c in range(4):
+                cols = slice(P * c, P * c + P)
+                nc.tensor.matmul(acc[:, cols], lhsT=first[:, cols], rhs=ident[:], is_transpose=True, start=True, stop=False)
+                nc.tensor.matmul(acc[:, cols], lhsT=second[:, cols], rhs=ident[:], is_transpose=True, start=False, stop=True)
+            return acc
+
+        three_s = pick(xs, l_three, V, U8, "three_s")
+        two_s = pick(xs, l_two, S, U8, "two_s")
+        offs_s = pick(xs, l_offs, S, U8, "offs_s")
+
+        w3_bf = sb([P, 4, P, 4], BF16, "w3_bf")
+        for h, engine_copy in enumerate((nc.vector.tensor_copy, nc.vector.tensor_copy)):
+            engine_copy(w3_bf[:, :, 64 * h : 64 * h + 64, :].rearrange("p t m j -> p m j t"), w3_raw[h][:].rearrange("p j (m t) -> p m j t", t=4))
+        w3_q = quantise(w3_bf[:].rearrange("p t m j -> p (t m j)"), "w3_q")
+        x_three = (pick(xw, l_three, V, U32, "three_w"), three_s)
+        for t in range(4):
+            b = bank(V, f"b{t}", t)
+            product(b[:], w3_q, P * t, x_three)
+            nc.scalar.activation(g_win[t][:, :V], b[:], ACT.Sigmoid)
+            nc.scalar.copy(b_win[t][:, :V], b[:])
+
+        z2_planes = sb([P, 4, V], BF16, "z2_planes")
+        fetched = [sb([P, 3, V], F32, f"fetched{t}") for t in range(4)]
+
+        def fetch_b(t):
+            nc.scalar.activation(fetched[t][:, 0, :], b_win[t][:].indirect(l_n3[:]), ACT.Copy)
+            nc.scalar.activation(fetched[t][:, 1, :], b_win[t][:].indirect(l_n4[:]), ACT.Copy)
+            nc.scalar.activation(fetched[t][:, 2, :], g_win[t][:].indirect(l_n5[:]), ACT.Copy)
+
+        def combine_b(t):
+            terms = sb([P, 2, V], F32, f"terms{t}")
+            nc.vector.scalar_tensor_tensor(terms[:, 0, :], fetched[t][:, 0, :], gb_t[:, t : t + 1], g_win[t][:, :V], ALU.mult, ALU.mult)
+            nc.vector.scalar_tensor_tensor(terms[:, 1, :], fetched[t][:, 1, :], gb_t[:, t : t + 1], fetched[t][:, 2, :], ALU.mult, ALU.mult)
+            nc.vector.tensor_tensor(z2_planes[:, t, :], terms[:, 0, :], terms[:, 1, :], ALU.add)
+
+        for t in range(2):
+            fetch_b(t)
+
+        x_two = (pick(xw, l_two, S, U32, "two_w"), two_s)
+        w2_q = quantise(cast_plain(nc.vector.tensor_copy, w2_raw, "w2_bf"), "w2_q")
+        x_offs = (pick(xw, l_offs, S, U32, "offs_w"), offs_s)
+        w1_q = quantise(cast_plain(nc.vector.tensor_copy, w1_raw, "w1_bf"), "w1_q")
+        for t in range(4):
+            d = bank(S, f"d{t}", 4 + t)
+            product(d[:], w2_q, P * t, x_two)
+            nc.scalar.activation(a_win[t][:, :S], d[:], ACT.Abs)
+        z_rows = sb([P, 4, H], BF16, "z_rows")
+        a_n2 = [sb([P, S], F32, f"a_n2_{t}") for t in range(4)]
+        y_n1 = [sb([P, S], F32, f"y_n1_{t}") for t in range(4)]
+        for t in range(4):
+            y = bank(S, f"y{t}", t)
+            product(y[:], w1_q, P * t, x_offs)
+            nc.vector.tensor_scalar(y_win[t][:, :S], y[:], ga_t[:, t : t + 1], None, ALU.mult)
+            nc.scalar.activation(y_n1[t][:], y_win[t][:].indirect(l_n1[:]), ACT.Copy, scale=-1.0)
+            nc.vector.tensor_copy(a_n2[t][:], a_win[t][:].indirect(l_n2[:]))
+            den = turn_and_add(a_win[t], a_n2[t], f"den{t}", 4 + t)
+            root = sb([P, S], F32, f"root{t}")
+            nc.scalar.activation(root[:], den[:], ACT.Abs_reciprocal_sqrt, bias=half[:])
+            diff = turn_and_add(y_win[t], y_n1[t], f"diff{t}", t)
+            once = sb([P, S], F32, f"once{t}")
+            nc.vector.tensor_tensor(once[:], diff[:], root[:], ALU.mult)
+            nc.vector.tensor_tensor(z_rows[:, :, P * t : P * t + P], once[:].rearrange("p (c i) -> p c i", c=4),
+                                    root[:].rearrange("p (c i) -> p c i", c=4), ALU.mult)
+        for t in range(2, 4):
+            fetch_b(t)
+
+        z_words = z_rows[:].rearrange("p c i -> p (c i)").bitcast(F32)
+        z_bf = sb([P, 4 * S], BF16, "z_bf")
+        z_bf_words = z_bf[:].bitcast(F32).rearrange("p (t m u) -> p t m u", t=4, u=2)
+        for h, engine_copy in enumerate((nc.scalar.copy, nc.scalar.copy)):
+            back = bank(S, f"back{h}", 4 + h)
+            for u in range(2):
+                for c2 in range(2):
+                    c = 2 * h + c2
+                    col = 256 * u + P * c2
+                    nc.tensor.transpose(back[:, col : col + P], z_words[:, 256 * c + u : 256 * (c + 1) : 2], ident[:])
+            engine_copy(z_bf_words[:, :, 64 * h : 64 * h + 64, :], back[:].rearrange("p (u m t) -> p t m u", u=2, t=4))
+        z_q = quantise(z_bf[:], "z_q")
+
+        for t in range(4):
+            combine_b(t)
+        z2_bf = sb([P, V, 4], BF16, "z2_bf")
+        nc.vector.tensor_copy(z2_bf[:].rearrange("p (c i) j -> p c j i", i=4), z2_planes[:].rearrange("p j (c i) -> p c j i", i=4))
+        z2_q = quantise(z2_bf[:].rearrange("p c j -> p (c j)"), "z2_q")
+
+        tab_n7 = sb([P, 4, V], F32, "tab_n7", tag="z2_bf")
+        for t in range(4):
+            nc.vector.tensor_copy(tab_n7[:, t, :], tab_t[t][:].indirect(l_n7[:]))
+        for t in range(4):
+            s = bank(V, f"s{t}", t)
+            product(s[:], z_q, P * t, z2_q)
+            nc.scalar.activation(s_win[t][:, :V], s[:], ACT.Copy, scale=0.0625)
+            s_n8 = sb([P, V], F32, f"s_n8_{t}")
+            nc.scalar.activation(s_n8[:], s_win[t][:].indirect(l_n8[:]), ACT.Copy)
+            scaled = sb([P, V], F32, f"scaled{t}")
+            nc.vector.tensor_tensor(scaled[:], tab_t[t][:].indirect(l_n6[:]), s_n8[:], ALU.mult)
+            result = sb([P, V], F32, f"result{t}")
+            nc.vector.tensor_tensor(result[:], tab_n7[:, t, :], scaled[:], ALU.add)
+            nc.sync.dma_start(out.rearrange("(p t) v -> t p v", t=4)[t], result[:])

@@ -45,9 +45,9 @@ def tile_picked_twknormbwsumkinda_none_p_kernel(tc, x_words, x_scales, w1, w2, w
             return raw
 
         xs = sb([P, T], U8, "xs")
-        nc.vector.memset(xs[:].bitcast(I32), 0)
         for q in range(4):
-            nc.scalar.dma_start(xs[32 * q : 32 * q + 4, :].bitcast(I32), x_scales[0, 4 * q : 4 * q + 4, :].bitcast(I32))
+            rows = x_scales[0, 4 * q : 4 * q + 4, :].bitcast(I32)
+            nc.sync.dma_start(xs[32 * q : 32 * q + 32, :].bitcast(I32), rows.unsqueeze(0).to_broadcast([8, 4, T // 4]))
         l_three = load_list(three, "l_three")
         l_two = load_list(two, "l_two")
         l_offs = load_list(offs, "l_offs")
@@ -58,22 +58,22 @@ def tile_picked_twknormbwsumkinda_none_p_kernel(tc, x_words, x_scales, w1, w2, w
         l_n4 = load_list(n4, "l_n4")
         l_n5 = load_list(n5, "l_n5")
         w2_raw = load_weight(w2, 0, H, "w2_raw")
-        gb_t = sb([P, 4], F32, "gb_t")
-        nc.sync.dma_start(gb_t[:], gb.rearrange("(p t) o -> p (t o)", t=4))
-        w1_raw = load_weight(w1, 0, H, "w1_raw")
         l_n2 = load_list(n2, "l_n2")
         l_n1 = load_list(n1, "l_n1")
         ga_t = sb([P, 4], F32, "ga_t")
         with nc.allow_non_contiguous_dma(reason="one gain a partition"):
             nc.sync.dma_start(ga_t[:], ga.rearrange("(t p) o -> p (t o)", p=P))
+        gb_t = sb([P, 4], F32, "gb_t")
+        nc.sync.dma_start(gb_t[:], gb.rearrange("(p t) o -> p (t o)", t=4))
+        w1_raw = load_weight(w1, 0, H, "w1_raw")
         tab_t = []
         for t in range(4):
             rows = sb([P, J], F32, f"tab{t}")
             nc.sync.dma_start(rows[:], tab.rearrange("(p t) c -> t p c", t=4)[t])
             tab_t.append(rows)
-        l_n8 = load_list(n8, "l_n8")
-        l_n6 = load_list(n6, "l_n6")
         l_n7 = load_list(n7, "l_n7")
+        l_n6 = load_list(n6, "l_n6")
+        l_n8 = load_list(n8, "l_n8")
 
         a_win = [sb([P, A_WINDOW], F32, f"a_win{t}") for t in range(4)]
         y_win = [sb([P, Y_WINDOW], F32, f"y_win{t}") for t in range(4)]
@@ -100,7 +100,7 @@ def tile_picked_twknormbwsumkinda_none_p_kernel(tc, x_words, x_scales, w1, w2, w
         def cast_plain(engine_copy, raw, name):
             width = raw.shape[2]
             grouped = sb([P, width, 4], BF16, name)
-            engine_copy(grouped[:].rearrange("p (c i) j -> p c j i", i=4), raw[:].rearrange("p j (c i) -> p c j i", i=4))
+            engine_copy(grouped[:].rearrange("p (c i) j -> p c j i", i=4), raw.rearrange("p j (c i) -> p c j i", i=4))
             return grouped[:].rearrange("p c j -> p (c j)")
 
         def quantise(values, name):
@@ -127,7 +127,7 @@ def tile_picked_twknormbwsumkinda_none_p_kernel(tc, x_words, x_scales, w1, w2, w
         offs_s = pick(xs, l_offs, S, U8, "offs_s")
 
         w3_bf = sb([P, 4, P, 4], BF16, "w3_bf")
-        for h, engine_copy in enumerate((nc.vector.tensor_copy, nc.vector.tensor_copy)):
+        for h, engine_copy in enumerate((nc.scalar.copy, nc.vector.tensor_copy)):
             engine_copy(w3_bf[:, :, 64 * h : 64 * h + 64, :].rearrange("p t m j -> p m j t"), w3_raw[h][:].rearrange("p j (m t) -> p m j t", t=4))
         w3_q = quantise(w3_bf[:].rearrange("p t m j -> p (t m j)"), "w3_q")
         x_three = (pick(xw, l_three, V, U32, "three_w"), three_s)
@@ -138,49 +138,58 @@ def tile_picked_twknormbwsumkinda_none_p_kernel(tc, x_words, x_scales, w1, w2, w
             nc.scalar.copy(b_win[t][:, :V], b[:])
 
         z2_planes = sb([P, 4, V], BF16, "z2_planes")
-        fetched = [sb([P, 3, V], F32, f"fetched{t}") for t in range(4)]
 
-        def fetch_b(t):
-            nc.scalar.activation(fetched[t][:, 0, :], b_win[t][:].indirect(l_n3[:]), ACT.Copy)
-            nc.scalar.activation(fetched[t][:, 1, :], b_win[t][:].indirect(l_n4[:]), ACT.Copy)
-            nc.scalar.activation(fetched[t][:, 2, :], g_win[t][:].indirect(l_n5[:]), ACT.Copy)
+        def fetch_b(t, fetched):
+            nc.scalar.activation(fetched[:, 0, :], b_win[t][:].indirect(l_n3[:]), ACT.Copy)
+            nc.scalar.activation(fetched[:, 1, :], b_win[t][:].indirect(l_n4[:]), ACT.Copy)
+            nc.scalar.activation(fetched[:, 2, :], g_win[t][:].indirect(l_n5[:]), ACT.Copy)
 
-        def combine_b(t):
-            terms = sb([P, 2, V], F32, f"terms{t}")
-            nc.vector.scalar_tensor_tensor(terms[:, 0, :], fetched[t][:, 0, :], gb_t[:, t : t + 1], g_win[t][:, :V], ALU.mult, ALU.mult)
-            nc.vector.scalar_tensor_tensor(terms[:, 1, :], fetched[t][:, 1, :], gb_t[:, t : t + 1], fetched[t][:, 2, :], ALU.mult, ALU.mult)
+        def combine_b(t, fetched, tag):
+            terms = sb([P, 2, V], F32, f"terms{t}", tag)
+            nc.vector.scalar_tensor_tensor(terms[:, 0, :], fetched[:, 0, :], gb_t[:, t : t + 1], g_win[t][:, :V], ALU.mult, ALU.mult)
+            nc.vector.scalar_tensor_tensor(terms[:, 1, :], fetched[:, 1, :], gb_t[:, t : t + 1], fetched[:, 2, :], ALU.mult, ALU.mult)
             nc.vector.tensor_tensor(z2_planes[:, t, :], terms[:, 0, :], terms[:, 1, :], ALU.add)
 
+        early = [sb([P, 3, V], F32, f"early{t}") for t in range(2)]
         for t in range(2):
-            fetch_b(t)
+            fetch_b(t, early[t])
 
         x_two = (pick(xw, l_two, S, U32, "two_w"), two_s)
-        w2_q = quantise(cast_plain(nc.vector.tensor_copy, w2_raw, "w2_bf"), "w2_q")
+        w2_bf = [cast_plain(nc.vector.tensor_copy, w2_raw[:, :, 256 * h : 256 * h + 256], f"w2_bf{h}") for h in range(2)]
+        w2_q = [quantise(w2_bf[h], f"w2_q{h}") for h in range(2)]
         x_offs = (pick(xw, l_offs, S, U32, "offs_w"), offs_s)
-        w1_q = quantise(cast_plain(nc.vector.tensor_copy, w1_raw, "w1_bf"), "w1_q")
+        w1_bf = [cast_plain(nc.vector.tensor_copy, w1_raw[:, :, 256 * h : 256 * h + 256], f"w1_bf{h}") for h in range(2)]
+        w1_q = [quantise(w1_bf[h], f"w1_q{h}") for h in range(2)]
         for t in range(4):
             d = bank(S, f"d{t}", 4 + t)
-            product(d[:], w2_q, P * t, x_two)
+            product(d[:], w2_q[t // 2], P * (t % 2), x_two)
             nc.scalar.activation(a_win[t][:, :S], d[:], ACT.Abs)
+        for t in range(2):
+            combine_b(t, early[t], f"w1_bf{t % 2}")
         z_rows = sb([P, 4, H], BF16, "z_rows")
-        a_n2 = [sb([P, S], F32, f"a_n2_{t}") for t in range(4)]
-        y_n1 = [sb([P, S], F32, f"y_n1_{t}") for t in range(4)]
+        a_n2 = sb([P, 4, S], F32, "a_n2", "w1_raw")
+        y_n1 = {}
         for t in range(4):
             y = bank(S, f"y{t}", t)
-            product(y[:], w1_q, P * t, x_offs)
-            nc.vector.tensor_scalar(y_win[t][:, :S], y[:], ga_t[:, t : t + 1], None, ALU.mult)
+            product(y[:], w1_q[t // 2], P * (t % 2), x_offs)
+            if t in ():
+                nc.scalar.activation(y_win[t][:, :S], y[:], ACT.Copy, scale=ga_t[:, t : t + 1])
+            else:
+                nc.vector.tensor_scalar(y_win[t][:, :S], y[:], ga_t[:, t : t + 1], None, ALU.mult)
+            y_n1[t] = sb([P, S], F32, f"y_n1_{t}")
             nc.scalar.activation(y_n1[t][:], y_win[t][:].indirect(l_n1[:]), ACT.Copy, scale=-1.0)
-            nc.vector.tensor_copy(a_n2[t][:], a_win[t][:].indirect(l_n2[:]))
-            den = turn_and_add(a_win[t], a_n2[t], f"den{t}", 4 + t)
+            nc.vector.tensor_copy(a_n2[:, t, :], a_win[t][:].indirect(l_n2[:]))
+            den = turn_and_add(a_n2[:, t, :], a_win[t], f"den{t}", 4 + t)
             root = sb([P, S], F32, f"root{t}")
             nc.scalar.activation(root[:], den[:], ACT.Abs_reciprocal_sqrt, bias=half[:])
-            diff = turn_and_add(y_win[t], y_n1[t], f"diff{t}", t)
+            diff = turn_and_add(y_n1[t], y_win[t], f"diff{t}", t)
             once = sb([P, S], F32, f"once{t}")
             nc.vector.tensor_tensor(once[:], diff[:], root[:], ALU.mult)
             nc.vector.tensor_tensor(z_rows[:, :, P * t : P * t + P], once[:].rearrange("p (c i) -> p c i", c=4),
                                     root[:].rearrange("p (c i) -> p c i", c=4), ALU.mult)
+        late = sb([P, 2, 3, V], F32, "late", "w1_raw")
         for t in range(2, 4):
-            fetch_b(t)
+            fetch_b(t, late[:, t - 2])
 
         z_words = z_rows[:].rearrange("p c i -> p (c i)").bitcast(F32)
         z_bf = sb([P, 4 * S], BF16, "z_bf")
@@ -195,15 +204,18 @@ def tile_picked_twknormbwsumkinda_none_p_kernel(tc, x_words, x_scales, w1, w2, w
             engine_copy(z_bf_words[:, :, 64 * h : 64 * h + 64, :], back[:].rearrange("p (u m t) -> p t m u", u=2, t=4))
         z_q = quantise(z_bf[:], "z_q")
 
-        for t in range(4):
-            combine_b(t)
+        for t in range(2, 4):
+            combine_b(t, late[:, t - 2], "")
         z2_bf = sb([P, V, 4], BF16, "z2_bf")
         nc.vector.tensor_copy(z2_bf[:].rearrange("p (c i) j -> p c j i", i=4), z2_planes[:].rearrange("p j (c i) -> p c j i", i=4))
         z2_q = quantise(z2_bf[:].rearrange("p c j -> p (c j)"), "z2_q")
 
-        tab_n7 = sb([P, 4, V], F32, "tab_n7", tag="z2_bf")
+        tab_n7 = sb([P, 4, V], F32, "tab_n7", "z2_bf")
         for t in range(4):
             nc.vector.tensor_copy(tab_n7[:, t, :], tab_t[t][:].indirect(l_n7[:]))
+        tab_n6 = sb([P, 4, V], F32, "tab_n6", "z_rows")
+        for t in range(4):
+            nc.scalar.activation(tab_n6[:, t, :], tab_t[t][:].indirect(l_n6[:]), ACT.Copy)
         for t in range(4):
             s = bank(V, f"s{t}", t)
             product(s[:], z_q, P * t, z2_q)
@@ -211,7 +223,7 @@ def tile_picked_twknormbwsumkinda_none_p_kernel(tc, x_words, x_scales, w1, w2, w
             s_n8 = sb([P, V], F32, f"s_n8_{t}")
             nc.scalar.activation(s_n8[:], s_win[t][:].indirect(l_n8[:]), ACT.Copy)
             scaled = sb([P, V], F32, f"scaled{t}")
-            nc.vector.tensor_tensor(scaled[:], tab_t[t][:].indirect(l_n6[:]), s_n8[:], ALU.mult)
+            nc.vector.tensor_tensor(scaled[:], tab_n6[:, t, :], s_n8[:], ALU.mult)
             result = sb([P, V], F32, f"result{t}")
             nc.vector.tensor_tensor(result[:], tab_n7[:, t, :], scaled[:], ALU.add)
             nc.sync.dma_start(out.rearrange("(p t) v -> t p v", t=4)[t], result[:])

@@ -58,14 +58,14 @@ def tile_picked_twknormbwsumkinda_none_p_kernel(tc, x_words, x_scales, w1, w2, w
         l_n4 = load_list(n4, "l_n4")
         l_n5 = load_list(n5, "l_n5")
         w2_raw = load_weight(w2, 0, H, "w2_raw")
-        l_n2 = load_list(n2, "l_n2")
-        l_n1 = load_list(n1, "l_n1")
-        ga_t = sb([P, 4], F32, "ga_t")
-        with nc.allow_non_contiguous_dma(reason="one gain a partition"):
-            nc.sync.dma_start(ga_t[:], ga.rearrange("(t p) o -> p (t o)", p=P))
         gb_t = sb([P, 4], F32, "gb_t")
         nc.sync.dma_start(gb_t[:], gb.rearrange("(p t) o -> p (t o)", t=4))
         w1_raw = load_weight(w1, 0, H, "w1_raw")
+        ga_t = sb([P, 4], F32, "ga_t")
+        with nc.allow_non_contiguous_dma(reason="one gain a partition"):
+            nc.sync.dma_start(ga_t[:], ga.rearrange("(t p) o -> p (t o)", p=P))
+        l_n2 = load_list(n2, "l_n2")
+        l_n1 = load_list(n1, "l_n1")
         tab_t = []
         for t in range(4):
             rows = sb([P, J], F32, f"tab{t}")
@@ -78,15 +78,12 @@ def tile_picked_twknormbwsumkinda_none_p_kernel(tc, x_words, x_scales, w1, w2, w
         a_win = [sb([P, A_WINDOW], F32, f"a_win{t}") for t in range(4)]
         y_win = [sb([P, Y_WINDOW], F32, f"y_win{t}") for t in range(4)]
         b_win = [sb([P, 2 * V], F32, f"b_win{t}") for t in range(4)]
-        g_win = [sb([P, 2 * V], F32, f"g_win{t}") for t in range(4)]
+        g_win = {t: sb([P, 2 * V], F32, f"g_win{t}") for t in (2, 3)}
         s_win = [sb([P, 2 * V], F32, f"s_win{t}") for t in range(4)]
         for t in range(4):
-            nc.gpsimd.memset(b_win[t][:, V:], 0.0)
-            nc.gpsimd.memset(g_win[t][:, V:], 0.0)
-        for t in range(4):
-            nc.gpsimd.memset(a_win[t][:, S:], 0.0)
-            nc.gpsimd.memset(y_win[t][:, S:], 0.0)
-            nc.gpsimd.memset(s_win[t][:, V:], 0.0)
+            nc.vector.memset(a_win[t][:, S:], 0.0)
+            nc.vector.memset(y_win[t][:, S:], 0.0)
+            nc.vector.memset(s_win[t][:, V:], 0.0)
         ident = sb([P, P], F32, "ident")
         make_identity(nc, ident[:])
         half = sb([P, 1], F32, "half")
@@ -114,13 +111,11 @@ def tile_picked_twknormbwsumkinda_none_p_kernel(tc, x_words, x_scales, w1, w2, w
             nc.tensor.matmul_mx(out=acc, lhsT=stat[0][:, c0 : c0 + P].bitcast(FP8X4), lhsT_scale=stat[1][:, c0 : c0 + P],
                                 rhs=mov[0][:].bitcast(FP8X4), rhs_scale=mov[1][:], start=True, stop=True)
 
-        def turn_and_add(first, second, name, index):
-            acc = bank(S, name, index)
+        def turn(acc, values, opens):
             for c in range(4):
                 cols = slice(P * c, P * c + P)
-                nc.tensor.matmul(acc[:, cols], lhsT=first[:, cols], rhs=ident[:], is_transpose=True, start=True, stop=False)
-                nc.tensor.matmul(acc[:, cols], lhsT=second[:, cols], rhs=ident[:], is_transpose=True, start=False, stop=True)
-            return acc
+                nc.tensor.matmul(acc[:, cols], lhsT=values[:, cols], rhs=ident[:], is_transpose=True,
+                                 start=opens and c == 0, stop=not opens and c == 3)
 
         three_s = pick(xs, l_three, V, U8, "three_s")
         two_s = pick(xs, l_two, S, U8, "two_s")
@@ -131,26 +126,30 @@ def tile_picked_twknormbwsumkinda_none_p_kernel(tc, x_words, x_scales, w1, w2, w
             engine_copy(w3_bf[:, :, 64 * h : 64 * h + 64, :].rearrange("p t m j -> p m j t"), w3_raw[h][:].rearrange("p j (m t) -> p m j t", t=4))
         w3_q = quantise(w3_bf[:].rearrange("p t m j -> p (t m j)"), "w3_q")
         x_three = (pick(xw, l_three, V, U32, "three_w"), three_s)
+        gate = [b_win[0][:, V:], b_win[1][:, V:], g_win[2][:, :V], g_win[3][:, :V]]
         for t in range(4):
             b = bank(V, f"b{t}", t)
             product(b[:], w3_q, P * t, x_three)
-            nc.scalar.activation(g_win[t][:, :V], b[:], ACT.Sigmoid)
+            nc.scalar.activation(gate[t], b[:], ACT.Sigmoid)
             nc.scalar.copy(b_win[t][:, :V], b[:])
 
         z2_planes = sb([P, 4, V], BF16, "z2_planes")
 
         def fetch_b(t, fetched):
-            nc.scalar.activation(fetched[:, 0, :], b_win[t][:].indirect(l_n3[:]), ACT.Copy)
-            nc.scalar.activation(fetched[:, 1, :], b_win[t][:].indirect(l_n4[:]), ACT.Copy)
-            nc.scalar.activation(fetched[:, 2, :], g_win[t][:].indirect(l_n5[:]), ACT.Copy)
+            nc.scalar.activation(fetched[0], b_win[t][:].indirect(l_n3[:]), ACT.Copy)
+            nc.scalar.activation(fetched[1], b_win[t][:].indirect(l_n4[:]), ACT.Copy)
+            if t < 2:
+                nc.scalar.activation(fetched[2], b_win[t][:].indirect(l_n5[:]), ACT.Sigmoid)
+            else:
+                nc.scalar.activation(fetched[2], g_win[t][:].indirect(l_n5[:]), ACT.Copy)
 
         def combine_b(t, fetched, tag):
             terms = sb([P, 2, V], F32, f"terms{t}", tag)
-            nc.vector.scalar_tensor_tensor(terms[:, 0, :], fetched[:, 0, :], gb_t[:, t : t + 1], g_win[t][:, :V], ALU.mult, ALU.mult)
-            nc.vector.scalar_tensor_tensor(terms[:, 1, :], fetched[:, 1, :], gb_t[:, t : t + 1], fetched[:, 2, :], ALU.mult, ALU.mult)
+            nc.vector.scalar_tensor_tensor(terms[:, 0, :], fetched[0], gb_t[:, t : t + 1], gate[t], ALU.mult, ALU.mult)
+            nc.vector.scalar_tensor_tensor(terms[:, 1, :], fetched[1], gb_t[:, t : t + 1], fetched[2], ALU.mult, ALU.mult)
             nc.vector.tensor_tensor(z2_planes[:, t, :], terms[:, 0, :], terms[:, 1, :], ALU.add)
 
-        early = [sb([P, 3, V], F32, f"early{t}") for t in range(2)]
+        early = [(b_win[2 + t][:, V:], g_win[2 + t][:, V:], sb([P, V], F32, f"early{t}")[:]) for t in range(2)]
         for t in range(2):
             fetch_b(t, early[t])
 
@@ -160,15 +159,20 @@ def tile_picked_twknormbwsumkinda_none_p_kernel(tc, x_words, x_scales, w1, w2, w
         x_offs = (pick(xw, l_offs, S, U32, "offs_w"), offs_s)
         w1_bf = [cast_plain(nc.vector.tensor_copy, w1_raw[:, :, 256 * h : 256 * h + 256], f"w1_bf{h}") for h in range(2)]
         w1_q = [quantise(w1_bf[h], f"w1_q{h}") for h in range(2)]
+        den = {}
+        diff = {}
         for t in range(4):
             d = bank(S, f"d{t}", 4 + t)
             product(d[:], w2_q[t // 2], P * (t % 2), x_two)
             nc.scalar.activation(a_win[t][:, :S], d[:], ACT.Abs)
-        for t in range(2):
-            combine_b(t, early[t], f"w1_bf{t % 2}")
         z_rows = sb([P, 4, H], BF16, "z_rows")
-        a_n2 = sb([P, 4, S], F32, "a_n2", "w1_raw")
+        a_n2 = sb([P, 4, S], F32, "a_n2", "w1_q1_w")
         y_n1 = {}
+
+        def fetch_y(t):
+            y_n1[t] = sb([P, S], F32, f"y_n1_{t}", f"y_n1_{t % 2}")
+            nc.scalar.activation(y_n1[t][:], y_win[t][:].indirect(l_n1[:]), ACT.Copy, scale=-1.0)
+
         for t in range(4):
             y = bank(S, f"y{t}", t)
             product(y[:], w1_q[t // 2], P * (t % 2), x_offs)
@@ -176,39 +180,49 @@ def tile_picked_twknormbwsumkinda_none_p_kernel(tc, x_words, x_scales, w1, w2, w
                 nc.scalar.activation(y_win[t][:, :S], y[:], ACT.Copy, scale=ga_t[:, t : t + 1])
             else:
                 nc.vector.tensor_scalar(y_win[t][:, :S], y[:], ga_t[:, t : t + 1], None, ALU.mult)
-            y_n1[t] = sb([P, S], F32, f"y_n1_{t}")
-            nc.scalar.activation(y_n1[t][:], y_win[t][:].indirect(l_n1[:]), ACT.Copy, scale=-1.0)
+            diff[t] = bank(S, f"diff{t}", 4 + t)
+            turn(diff[t], y_win[t], True)
+            den[t] = bank(S, f"den{t}", t)
+            turn(den[t], a_win[t], True)
+            if t < 2:
+                fetch_y(t)
+        for t in range(4):
             nc.vector.tensor_copy(a_n2[:, t, :], a_win[t][:].indirect(l_n2[:]))
-            den = turn_and_add(a_n2[:, t, :], a_win[t], f"den{t}", 4 + t)
+        for t in range(2):
+            combine_b(t, early[t], f"w1_bf{t % 2}")
+        for t in range(4):
+            turn(den[t], a_n2[:, t, :], False)
             root = sb([P, S], F32, f"root{t}")
-            nc.scalar.activation(root[:], den[:], ACT.Abs_reciprocal_sqrt, bias=half[:])
-            diff = turn_and_add(y_n1[t], y_win[t], f"diff{t}", t)
+            nc.scalar.activation(root[:], den[t][:], ACT.Abs_reciprocal_sqrt, bias=half[:])
+            turn(diff[t], y_n1[t], False)
+            if t < 2:
+                fetch_y(t + 2)
             once = sb([P, S], F32, f"once{t}")
-            nc.vector.tensor_tensor(once[:], diff[:], root[:], ALU.mult)
+            nc.vector.tensor_tensor(once[:], diff[t][:], root[:], ALU.mult)
             nc.vector.tensor_tensor(z_rows[:, :, P * t : P * t + P], once[:].rearrange("p (c i) -> p c i", c=4),
                                     root[:].rearrange("p (c i) -> p c i", c=4), ALU.mult)
-        late = sb([P, 2, 3, V], F32, "late", "w1_raw")
+        late = sb([P, 2, 3, V], F32, "late", "w1_q1_w")
         for t in range(2, 4):
-            fetch_b(t, late[:, t - 2])
+            fetch_b(t, [late[:, t - 2, k, :] for k in range(3)])
 
         z_words = z_rows[:].rearrange("p c i -> p (c i)").bitcast(F32)
         z_bf = sb([P, 4 * S], BF16, "z_bf")
         z_bf_words = z_bf[:].bitcast(F32).rearrange("p (t m u) -> p t m u", t=4, u=2)
         for h, engine_copy in enumerate((nc.scalar.copy, nc.scalar.copy)):
-            back = bank(S, f"back{h}", 4 + h)
+            back = bank(S, f"back{h}", h)
             for u in range(2):
                 for c2 in range(2):
                     c = 2 * h + c2
                     col = 256 * u + P * c2
                     nc.tensor.transpose(back[:, col : col + P], z_words[:, 256 * c + u : 256 * (c + 1) : 2], ident[:])
             engine_copy(z_bf_words[:, :, 64 * h : 64 * h + 64, :], back[:].rearrange("p (u m t) -> p t m u", u=2, t=4))
-        z_q = quantise(z_bf[:], "z_q")
 
         for t in range(2, 4):
-            combine_b(t, late[:, t - 2], "")
+            combine_b(t, [late[:, t - 2, k, :] for k in range(3)], "")
         z2_bf = sb([P, V, 4], BF16, "z2_bf")
         nc.vector.tensor_copy(z2_bf[:].rearrange("p (c i) j -> p c j i", i=4), z2_planes[:].rearrange("p j (c i) -> p c j i", i=4))
         z2_q = quantise(z2_bf[:].rearrange("p c j -> p (c j)"), "z2_q")
+        z_q = [quantise(z_bf[:, 512 * h : 512 * (h + 1)], f"z_q{h}") for h in range(4)]
 
         tab_n7 = sb([P, 4, V], F32, "tab_n7", "z2_bf")
         for t in range(4):
@@ -217,8 +231,8 @@ def tile_picked_twknormbwsumkinda_none_p_kernel(tc, x_words, x_scales, w1, w2, w
         for t in range(4):
             nc.scalar.activation(tab_n6[:, t, :], tab_t[t][:].indirect(l_n6[:]), ACT.Copy)
         for t in range(4):
-            s = bank(V, f"s{t}", t)
-            product(s[:], z_q, P * t, z2_q)
+            s = bank(V, f"s{t}", 4 + t)
+            product(s[:], z_q[t], 0, z2_q)
             nc.scalar.activation(s_win[t][:, :V], s[:], ACT.Copy, scale=0.0625)
             s_n8 = sb([P, V], F32, f"s_n8_{t}")
             nc.scalar.activation(s_n8[:], s_win[t][:].indirect(l_n8[:]), ACT.Copy)

@@ -133,7 +133,7 @@ def tile_picked_twknormbwsumkinda_none_p_kernel(tc, x_words, x_scales, w1, w2, w
             nc.scalar.activation(gate[t], b[:], ACT.Sigmoid)
             nc.scalar.copy(b_win[t][:, :V], b[:])
 
-        z2_planes = sb([P, 4, V], BF16, "z2_planes")
+        z2_bf = sb([P, V, 2, 2], BF16, "z2_bf")
 
         def fetch_b(t, fetched):
             nc.scalar.activation(fetched[0], b_win[t][:].indirect(l_n3[:]), ACT.Copy)
@@ -143,11 +143,13 @@ def tile_picked_twknormbwsumkinda_none_p_kernel(tc, x_words, x_scales, w1, w2, w
             else:
                 nc.scalar.activation(fetched[2], g_win[t][:].indirect(l_n5[:]), ACT.Copy)
 
-        def combine_b(t, fetched, tag):
-            terms = sb([P, 2, V], F32, f"terms{t}", tag)
-            nc.vector.scalar_tensor_tensor(terms[:, 0, :], fetched[0], gb_t[:, t : t + 1], gate[t], ALU.mult, ALU.mult)
-            nc.vector.scalar_tensor_tensor(terms[:, 1, :], fetched[1], gb_t[:, t : t + 1], fetched[2], ALU.mult, ALU.mult)
-            nc.vector.tensor_tensor(z2_planes[:, t, :], terms[:, 0, :], terms[:, 1, :], ALU.add)
+        def combine_b(u, fetched, tag):
+            terms = sb([P, 2, 2, V], F32, f"terms{u}", tag)
+            for e in range(2):
+                t = 2 * u + e
+                nc.vector.scalar_tensor_tensor(terms[:, 0, e, :], fetched[e][0], gb_t[:, t : t + 1], gate[t], ALU.mult, ALU.mult)
+                nc.vector.scalar_tensor_tensor(terms[:, 1, e, :], fetched[e][1], gb_t[:, t : t + 1], fetched[e][2], ALU.mult, ALU.mult)
+            nc.vector.tensor_tensor(z2_bf[:, :, u, :], terms[:, 0].rearrange("p e v -> p v e"), terms[:, 1].rearrange("p e v -> p v e"), ALU.add)
 
         early = [(b_win[2 + t][:, V:], g_win[2 + t][:, V:], sb([P, V], F32, f"early{t}")[:]) for t in range(2)]
         for t in range(2):
@@ -188,8 +190,7 @@ def tile_picked_twknormbwsumkinda_none_p_kernel(tc, x_words, x_scales, w1, w2, w
                 fetch_y(t)
         for t in range(4):
             nc.vector.tensor_copy(a_n2[:, t, :], a_win[t][:].indirect(l_n2[:]))
-        for t in range(2):
-            combine_b(t, early[t], f"w1_bf{t % 2}")
+        combine_b(0, early, "w1_bf0")
         for t in range(4):
             turn(den[t], a_n2[:, t, :], False)
             root = sb([P, S], F32, f"root{t}")
@@ -208,7 +209,7 @@ def tile_picked_twknormbwsumkinda_none_p_kernel(tc, x_words, x_scales, w1, w2, w
         z_words = z_rows[:].rearrange("p c i -> p (c i)").bitcast(F32)
         z_bf = sb([P, 4 * S], BF16, "z_bf")
         z_bf_words = z_bf[:].bitcast(F32).rearrange("p (t m u) -> p t m u", t=4, u=2)
-        for h, engine_copy in enumerate((nc.scalar.copy, nc.scalar.copy)):
+        for h, engine_copy in enumerate((nc.scalar.copy, nc.vector.tensor_copy)):
             back = bank(S, f"back{h}", h)
             for u in range(2):
                 for c2 in range(2):
@@ -217,11 +218,8 @@ def tile_picked_twknormbwsumkinda_none_p_kernel(tc, x_words, x_scales, w1, w2, w
                     nc.tensor.transpose(back[:, col : col + P], z_words[:, 256 * c + u : 256 * (c + 1) : 2], ident[:])
             engine_copy(z_bf_words[:, :, 64 * h : 64 * h + 64, :], back[:].rearrange("p (u m t) -> p t m u", u=2, t=4))
 
-        for t in range(2, 4):
-            combine_b(t, [late[:, t - 2, k, :] for k in range(3)], "")
-        z2_bf = sb([P, V, 4], BF16, "z2_bf")
-        nc.vector.tensor_copy(z2_bf[:].rearrange("p (c i) j -> p c j i", i=4), z2_planes[:].rearrange("p j (c i) -> p c j i", i=4))
-        z2_q = quantise(z2_bf[:].rearrange("p c j -> p (c j)"), "z2_q")
+        combine_b(1, [[late[:, e, k, :] for k in range(3)] for e in range(2)], "")
+        z2_q = quantise(z2_bf[:].rearrange("p v u e -> p (v u e)"), "z2_q")
         z_q = [quantise(z_bf[:, 512 * h : 512 * (h + 1)], f"z_q{h}") for h in range(4)]
 
         tab_n7 = sb([P, 4, V], F32, "tab_n7", "z2_bf")
@@ -235,9 +233,10 @@ def tile_picked_twknormbwsumkinda_none_p_kernel(tc, x_words, x_scales, w1, w2, w
             product(s[:], z_q[t], 0, z2_q)
             nc.scalar.activation(s_win[t][:, :V], s[:], ACT.Copy, scale=0.0625)
             s_n8 = sb([P, V], F32, f"s_n8_{t}")
-            nc.scalar.activation(s_n8[:], s_win[t][:].indirect(l_n8[:]), ACT.Copy)
             scaled = sb([P, V], F32, f"scaled{t}")
-            nc.vector.tensor_tensor(scaled[:], tab_n6[:, t, :], s_n8[:], ALU.mult)
             result = sb([P, V], F32, f"result{t}")
-            nc.vector.tensor_tensor(result[:], tab_n7[:, t, :], scaled[:], ALU.add)
-            nc.sync.dma_start(out.rearrange("(p t) v -> t p v", t=4)[t], result[:])
+            for cols in ([slice(0, V)] if t < 3 else [slice(0, V // 2), slice(V // 2, V)]):
+                nc.scalar.activation(s_n8[:, cols], s_win[t][:].indirect(l_n8[:, cols.start // 16 : cols.stop // 16]), ACT.Copy)
+                nc.vector.tensor_tensor(scaled[:, cols], tab_n6[:, t, cols], s_n8[:, cols], ALU.mult)
+                nc.vector.tensor_tensor(result[:, cols], tab_n7[:, t, cols], scaled[:, cols], ALU.add)
+                nc.sync.dma_start(out.rearrange("(p t) v -> t p v", t=4)[t][:, cols], result[:, cols])

from contextlib import ExitStack

import concourse.mybir as mybir
from concourse.masks import make_identity

F32 = mybir.dt.float32
BF16 = mybir.dt.bfloat16
I32 = mybir.dt.int32
U32 = mybir.dt.uint32
U16 = mybir.dt.uint16
U8 = mybir.dt.uint8
FP8X4 = mybir.dt.float8_e4m3fn_x4
ACT = mybir.ActivationFunctionType
ALU = mybir.AluOpType

K, T, S, V, H, J = 512, 2048, 512, 256, 512, 512
P = 128
FLOPS = 2 * K * H * (S + S + V) + 2 * H * S * V

Y_WINDOW = S + 16
A_WINDOW = S + 192


def tile_picked_twknormbwsumkinda_none_p_kernel(tc, x_words, x_scales, w1, w2, w3, ga, gb, tab, offs, two, n1, n2, three, n3, n4, n5, n6, n7, n8, out):
    nc = tc.nc
    with ExitStack() as ctx:
        lists = ctx.enter_context(tc.tile_pool(name="lists", bufs=1))
        keep = ctx.enter_context(tc.tile_pool(name="keep", bufs=1))
        psum = ctx.enter_context(tc.psum_pool(name="psum", bufs=1))

        def load_list(src, name):
            lst = lists.tile([P, src.shape[1]], U16, name=name)
            nc.sync.dma_start(lst[:], src)
            return lst

        def sb(shape, dtype, name, tag=""):
            return keep.tile(shape, dtype, name=name, tag=tag or name, align_bytes=64)

        def bank(width, name, index):
            return psum.tile([P, width], F32, name=name, tag=f"bank{index}")

        def load_weight(w, c0, c1, name):
            raw = sb([P, 4, c1 - c0], F32, name)
            nc.sync.dma_start(raw[:], w.rearrange("(p j) c -> p j c", j=4)[:, :, c0:c1])
            return raw

        xs = sb([P, T], U8, "xs")
        for q in range(4):
            rows = x_scales[0, 4 * q : 4 * q + 4, :].bitcast(I32)
            nc.sync.dma_start(xs[32 * q : 32 * q + 32, :].bitcast(I32), rows.unsqueeze(0).to_broadcast([8, 4, T // 4]))
        l_three = load_list(three, "l_three")
        l_two = load_list(two, "l_two")
        l_offs = load_list(offs, "l_offs")
        w3_raw = [load_weight(w3, 256 * h, 256 * h + 256, f"w3_raw{h}") for h in range(2)]
        xw = sb([P, T], U32, "xw")
        nc.sync.dma_start(xw[:].bitcast(I32), x_words[0].rearrange("p n t -> p (n t)").bitcast(I32))
        l_n3 = load_list(n3, "l_n3")
        l_n4 = load_list(n4, "l_n4")
        l_n5 = load_list(n5, "l_n5")
        w2_raw = load_weight(w2, 0, H, "w2_raw")
        gb_t = sb([P, 4], F32, "gb_t")
        nc.sync.dma_start(gb_t[:], gb.rearrange("(p t) o -> p (t o)", t=4))
        w1_raw = load_weight(w1, 0, H, "w1_raw")
        ga_t = sb([P, 4], F32, "ga_t")
        with nc.allow_non_contiguous_dma(reason="one gain a partition"):
            nc.sync.dma_start(ga_t[:], ga.rearrange("(t p) o -> p (t o)", p=P))
        l_n2 = load_list(n2, "l_n2")
        l_n1 = load_list(n1, "l_n1")
        tab_t = []
        for t in range(4):
            rows = sb([P, J], F32, f"tab{t}")
            nc.sync.dma_start(rows[:], tab.rearrange("(p t) c -> t p c", t=4)[t])
            tab_t.append(rows)
        l_n7 = load_list(n7, "l_n7")
        l_n6 = load_list(n6, "l_n6")
        l_n8 = load_list(n8, "l_n8")

        a_win = [sb([P, A_WINDOW], F32, f"a_win{t}") for t in range(4)]
        y_win = [sb([P, Y_WINDOW], F32, f"y_win{t}") for t in range(4)]
        b_win = [sb([P, 2 * V], F32, f"b_win{t}") for t in range(4)]
        g_win = {t: sb([P, 2 * V], F32, f"g_win{t}") for t in (2, 3)}
        s_win = [sb([P, 2 * V], F32, f"s_win{t}") for t in range(4)]
        for t in range(4):
            nc.vector.memset(a_win[t][:, S:], 0.0)
            nc.vector.memset(y_win[t][:, S:], 0.0)
            nc.vector.memset(s_win[t][:, V:], 0.0)
        ident = sb([P, P], F32, "ident")
        make_identity(nc, ident[:])
        half = sb([P, 1], F32, "half")
        nc.gpsimd.memset(half[:], 0.5)

        def pick(table, lst, n, dtype, name):
            picked_bytes = sb([P, n], dtype, name)
            nc.vector.tensor_copy(picked_bytes[:], table[:].indirect(lst[:]))
            return picked_bytes

        def cast_plain(engine_copy, raw, name):
            width = raw.shape[2]
            grouped = sb([P, width, 4], BF16, name)
            engine_copy(grouped[:].rearrange("p (c i) j -> p c j i", i=4), raw.rearrange("p j (c i) -> p c j i", i=4))
            return grouped[:].rearrange("p c j -> p (c j)")

        def quantise(values, name):
            width = values.shape[1] // 4
            words = sb([P, width], U32, name + "_w")
            scales = sb([P, width], U8, name + "_s")
            nc.vector.quantize_mx(out=words[:].bitcast(FP8X4), scales=scales[:], in_=values)
            return words, scales

        def product(acc, stat, c0, mov):
            nc.tensor.matmul_mx(out=acc, lhsT=stat[0][:, c0 : c0 + P].bitcast(FP8X4), lhsT_scale=stat[1][:, c0 : c0 + P],
                                rhs=mov[0][:].bitcast(FP8X4), rhs_scale=mov[1][:], start=True, stop=True)

        def turn(acc, values, opens):
            for c in range(4):
                cols = slice(P * c, P * c + P)
                nc.tensor.matmul(acc[:, cols], lhsT=values[:, cols], rhs=ident[:], is_transpose=True,
                                 start=opens and c == 0, stop=not opens and c == 3)

        three_s = pick(xs, l_three, V, U8, "three_s")
        two_s = pick(xs, l_two, S, U8, "two_s")
        offs_s = pick(xs, l_offs, S, U8, "offs_s")

        w3_bf = sb([P, 4, P, 4], BF16, "w3_bf")
        for h, engine_copy in enumerate((nc.scalar.copy, nc.vector.tensor_copy)):
            engine_copy(w3_bf[:, :, 64 * h : 64 * h + 64, :].rearrange("p t m j -> p m j t"), w3_raw[h][:].rearrange("p j (m t) -> p m j t", t=4))
        w3_q = quantise(w3_bf[:].rearrange("p t m j -> p (t m j)"), "w3_q")
        x_three = (pick(xw, l_three, V, U32, "three_w"), three_s)
        gate = [b_win[0][:, V:], b_win[1][:, V:], g_win[2][:, :V], g_win[3][:, :V]]
        for t in range(4):
            b = bank(V, f"b{t}", t)
            product(b[:], w3_q, P * t, x_three)
            nc.scalar.activation(gate[t], b[:], ACT.Sigmoid)
            nc.scalar.copy(b_win[t][:, :V], b[:])

        z2_bf = sb([P, V, 2, 2], BF16, "z2_bf")

        def fetch_b(t, fetched):
            nc.scalar.activation(fetched[0], b_win[t][:].indirect(l_n3[:]), ACT.Copy)
            nc.scalar.activation(fetched[1], b_win[t][:].indirect(l_n4[:]), ACT.Copy)
            if t < 2:
                nc.scalar.activation(fetched[2], b_win[t][:].indirect(l_n5[:]), ACT.Sigmoid)
            else:
                nc.scalar.activation(fetched[2], g_win[t][:].indirect(l_n5[:]), ACT.Copy)

        def combine_b(u, fetched, tag):
            terms = sb([P, 2, 2, V], F32, f"terms{u}", tag)
            for e in range(2):
                t = 2 * u + e
                nc.vector.scalar_tensor_tensor(terms[:, 0, e, :], fetched[e][0], gb_t[:, t : t + 1], gate[t], ALU.mult, ALU.mult)
                nc.vector.scalar_tensor_tensor(terms[:, 1, e, :], fetched[e][1], gb_t[:, t : t + 1], fetched[e][2], ALU.mult, ALU.mult)
            nc.vector.tensor_tensor(z2_bf[:, :, u, :], terms[:, 0].rearrange("p e v -> p v e"), terms[:, 1].rearrange("p e v -> p v e"), ALU.add)

        early = [(b_win[2 + t][:, V:], g_win[2 + t][:, V:], sb([P, V], F32, f"early{t}")[:]) for t in range(2)]
        for t in range(2):
            fetch_b(t, early[t])

        x_two = (pick(xw, l_two, S, U32, "two_w"), two_s)
        w2_bf = [cast_plain(nc.vector.tensor_copy, w2_raw[:, :, 256 * h : 256 * h + 256], f"w2_bf{h}") for h in range(2)]
        w2_q = [quantise(w2_bf[h], f"w2_q{h}") for h in range(2)]
        x_offs = (pick(xw, l_offs, S, U32, "offs_w"), offs_s)
        w1_bf = [cast_plain(nc.vector.tensor_copy, w1_raw[:, :, 256 * h : 256 * h + 256], f"w1_bf{h}") for h in range(2)]
        w1_q = [quantise(w1_bf[h], f"w1_q{h}") for h in range(2)]
        den = {}
        diff = {}
        for t in range(4):
            d = bank(S, f"d{t}", 4 + t)
            product(d[:], w2_q[t // 2], P * (t % 2), x_two)
            nc.scalar.activation(a_win[t][:, :S], d[:], ACT.Abs)
        z_rows = sb([P, 4, H], BF16, "z_rows")
        a_n2 = sb([P, 4, S], F32, "a_n2", "w1_q1_w")
        y_n1 = {}

        def fetch_y(t):
            y_n1[t] = sb([P, S], F32, f"y_n1_{t}", f"y_n1_{t % 2}")
            nc.scalar.activation(y_n1[t][:], y_win[t][:].indirect(l_n1[:]), ACT.Copy, scale=-1.0)

        for t in range(4):
            y = bank(S, f"y{t}", t)
            product(y[:], w1_q[t // 2], P * (t % 2), x_offs)
            if t in ():
                nc.scalar.activation(y_win[t][:, :S], y[:], ACT.Copy, scale=ga_t[:, t : t + 1])
            else:
                nc.vector.tensor_scalar(y_win[t][:, :S], y[:], ga_t[:, t : t + 1], None, ALU.mult)
            diff[t] = bank(S, f"diff{t}", 4 + t)
            turn(diff[t], y_win[t], True)
            den[t] = bank(S, f"den{t}", t)
            turn(den[t], a_win[t], True)
            if t < 2:
                fetch_y(t)
        for t in range(4):
            nc.vector.tensor_copy(a_n2[:, t, :], a_win[t][:].indirect(l_n2[:]))
        combine_b(0, early, "w1_bf0")
        for t in range(4):
            turn(den[t], a_n2[:, t, :], False)
            root = sb([P, S], F32, f"root{t}")
            nc.scalar.activation(root[:], den[t][:], ACT.Abs_reciprocal_sqrt, bias=half[:])
            turn(diff[t], y_n1[t], False)
            if t < 2:
                fetch_y(t + 2)
            once = sb([P, S], F32, f"once{t}")
            nc.vector.tensor_tensor(once[:], diff[t][:], root[:], ALU.mult)
            nc.vector.tensor_tensor(z_rows[:, :, P * t : P * t + P], once[:].rearrange("p (c i) -> p c i", c=4),
                                    root[:].rearrange("p (c i) -> p c i", c=4), ALU.mult)
        late = sb([P, 2, 3, V], F32, "late", "w1_q1_w")
        for t in range(2, 4):
            fetch_b(t, [late[:, t - 2, k, :] for k in range(3)])

        z_words = z_rows[:].rearrange("p c i -> p (c i)").bitcast(F32)
        z_bf = sb([P, 4 * S], BF16, "z_bf")
        z_bf_words = z_bf[:].bitcast(F32).rearrange("p (t m u) -> p t m u", t=4, u=2)
        for h, engine_copy in enumerate((nc.scalar.copy, nc.vector.tensor_copy)):
            back = bank(S, f"back{h}", h)
            for u in range(2):
                for c2 in range(2):
                    c = 2 * h + c2
                    col = 256 * u + P * c2
                    nc.tensor.transpose(back[:, col : col + P], z_words[:, 256 * c + u : 256 * (c + 1) : 2], ident[:])
            engine_copy(z_bf_words[:, :, 64 * h : 64 * h + 64, :], back[:].rearrange("p (u m t) -> p t m u", u=2, t=4))

        combine_b(1, [[late[:, e, k, :] for k in range(3)] for e in range(2)], "")
        z2_q = quantise(z2_bf[:].rearrange("p v u e -> p (v u e)"), "z2_q")
        z_q = [quantise(z_bf[:, 512 * h : 512 * (h + 1)], f"z_q{h}") for h in range(4)]

        tab_n7 = sb([P, 4, V], F32, "tab_n7", "z2_bf")
        for t in range(4):
            nc.vector.tensor_copy(tab_n7[:, t, :], tab_t[t][:].indirect(l_n7[:]))
        tab_n6 = sb([P, 4, V], F32, "tab_n6", "z_rows")
        for t in range(4):
            nc.scalar.activation(tab_n6[:, t, :], tab_t[t][:].indirect(l_n6[:]), ACT.Copy)
        for t in range(4):
            s = bank(V, f"s{t}", 4 + t)
            product(s[:], z_q[t], 0, z2_q)
            nc.scalar.activation(s_win[t][:, :V], s[:], ACT.Copy, scale=0.0625)
            s_n8 = sb([P, V], F32, f"s_n8_{t}")
            scaled = sb([P, V], F32, f"scaled{t}")
            result = sb([P, V], F32, f"result{t}")
            for cols in ([slice(0, V)] if t < 3 else [slice(0, V // 2), slice(V // 2, V)]):
                nc.scalar.activation(s_n8[:, cols], s_win[t][:].indirect(l_n8[:, cols.start // 16 : cols.stop // 16]), ACT.Copy)
                nc.vector.tensor_tensor(scaled[:, cols], tab_n6[:, t, cols], s_n8[:, cols], ALU.mult)
                nc.vector.tensor_tensor(result[:, cols], tab_n7[:, t, cols], scaled[:, cols], ALU.add)
                nc.sync.dma_start(out.rearrange("(p t) v -> t p v", t=4)[t][:, cols], result[:, cols])
